import numpy as np
import ml_dtypes


def mxq(x, axis, fmt="e4m3"):
    dtype, down = {"e4m3": (ml_dtypes.float8_e4m3fn, 7), "e5m2": (ml_dtypes.float8_e5m2, 14)}[fmt]
    v = np.moveaxis(np.asarray(x, np.float32).astype(ml_dtypes.bfloat16).astype(np.float64), axis, -1)
    blocks = v.reshape(v.shape[:-1] + (-1, 32))
    amax = np.abs(blocks).max(-1, keepdims=True)
    byte = np.maximum(np.where(amax > 0, np.frexp(amax)[1] - 1 + 127, 0) - down, 1)
    scale = np.exp2(byte - 127.0)
    codes = (blocks / scale).astype(np.float32).astype(dtype).astype(np.float64)
    return np.moveaxis((codes * scale).reshape(v.shape), -1, axis)


WIDE = False


def mx_kscale(k):
    if not WIDE:
        return np.ones(k)
    levels = np.array([30, -30])
    if k % 512:
        return np.exp2(np.random.permutation(np.resize(levels, k // 32))).repeat(32)
    a = np.empty((k // 512, 16))
    for p in range(k // 512):
        a[p, :8] = np.random.permutation(np.resize(levels, 8))
        for g in range(8):
            far = levels[np.abs(levels - a[p, g]) >= 10]
            a[p, g + 8] = far[np.random.randint(len(far))]
    return np.exp2(a.ravel()).repeat(32)


def f64(x):
    return np.asarray(x).astype(np.float64)


def striped(idx):
    return np.tile(np.asarray(idx).reshape(-1, 16).T, (8, 1)).astype(np.uint16)


def unstriped(offs):
    return offs[:16].T.reshape(-1).astype(np.int64)


E2M1 = np.array([0.0, 0.5, 1.0, 1.5, 2.0, 3.0, 4.0, 6.0, -0.0, -0.5, -1.0, -1.5, -2.0, -3.0, -4.0, -6.0])


def pack_weight(w, fmt):
    k, n = w.shape
    w = f64(np.asarray(w, np.float32).astype(ml_dtypes.bfloat16)).reshape(k // 32, 32, n)
    amax = np.abs(w).max(1)
    if fmt in ("e4m3", "e5m2"):
        byte = np.frexp(amax)[1] - 1 + 127 - (7 if fmt == "e4m3" else 14)
    else:
        mant, ex = np.frexp(amax / 6.0)
        byte = np.where(mant > 0.5, ex, ex - 1) + 127
    byte = np.clip(np.where(amax > 0, byte, 1), 1, 254)
    scaled = (w * np.exp2(127.0 - byte)[:, None, :]).reshape(k, n).astype(np.float32)
    by_word = np.ascontiguousarray(scaled.reshape(k // 512, 128, 4, n).transpose(0, 1, 3, 2))
    if fmt in ("e4m3", "e5m2"):
        words = by_word.astype(ml_dtypes.float8_e4m3fn if fmt == "e4m3" else ml_dtypes.float8_e5m2).view(np.uint8)
    else:
        c = by_word.astype(ml_dtypes.float4_e2m1fn).view(np.uint8) & 0xF
        words = (c[..., 0::2] | (c[..., 1::2] << 4)).reshape(k // 512, 128, 2 * n)
    return np.ascontiguousarray(words), np.ascontiguousarray(byte.astype(np.uint8).reshape(k // 512, 16, n))


def unpack_weight(words, scales, fmt):
    g, _, n = scales.shape
    words = np.ascontiguousarray(words).reshape(g, 128, n, -1)
    if fmt in ("e4m3", "e5m2"):
        vals = words.view(ml_dtypes.float8_e4m3fn if fmt == "e4m3" else ml_dtypes.float8_e5m2).astype(np.float64)
    else:
        nib = np.empty((g, 128, n, 4), np.uint8)
        nib[..., 0::2] = words & 0xF
        nib[..., 1::2] = words >> 4
        vals = E2M1[nib]
    vals = vals * np.repeat(np.exp2(scales.astype(np.float64) - 127.0), 8, axis=1)[..., None]
    return vals.transpose(0, 1, 3, 2).reshape(g * 512, n)


K, T, J, R, C, N, E = 512, 2048, 256, 512, 512, 256, 1024


def setup_inputs():
    n = np.random.standard_normal
    idx = np.random.permutation(T)[:J]
    idx2 = np.random.permutation(T)[:J]
    idx3 = np.random.permutation(C)[:J]
    idx4 = np.random.permutation(C)[:J]
    idx5 = np.random.permutation(J)[:J]
    idx6 = np.random.permutation(E)[:J]
    fk = mx_kscale(K)
    fr = mx_kscale(R)
    xtp = pack_weight(n((K, T)) / fk[:, None], "e2m1")
    wp = pack_weight(n((K, R)) * 1 / np.sqrt(K) * fk[:, None] * fr, "e5m2")
    wbp = pack_weight(n((R, N)) * 1 / np.sqrt(R) / fr[:, None], "e4m3")
    wsp = pack_weight(n((K, N)) * 1 / np.sqrt(K) * fk[:, None], "e4m3")
    return {
        "xt_words": xtp[0],
        "xt_scales": xtp[1],
        "w_words": wp[0],
        "w_scales": wp[1],
        "wb_words": wbp[0],
        "wb_scales": wbp[1],
        "ws_words": wsp[0],
        "ws_scales": wsp[1],
        "offs": striped(idx),
        "offs2": striped(idx2),
        "offs3": striped(idx3),
        "offs4": striped(idx4),
        "offs5": striped(idx5),
        "offs6": striped(idx6),
    }


def reference(xt_words, xt_scales, w_words, w_scales, wb_words, wb_scales, ws_words, ws_scales, offs, offs2, offs3, offs4, offs5, offs6):
    idx = unstriped(offs)
    idx2 = unstriped(offs2)
    idx3 = unstriped(offs3)
    idx4 = unstriped(offs4)
    idx5 = unstriped(offs5)
    idx6 = unstriped(offs6)
    xtu = unpack_weight(xt_words, xt_scales, "e2m1")
    wu = unpack_weight(w_words, w_scales, "e5m2")
    wbu = unpack_weight(wb_words, wb_scales, "e4m3")
    wsu = unpack_weight(ws_words, ws_scales, "e4m3")
    xtidxg = xtu[:, idx]
    a = wu.T @ xtidxg
    xtidx2g = xtu[:, idx2]
    b = wu.T @ xtidx2g
    pw = np.zeros((R, C))
    pw[:, idx3] = a
    hid = np.maximum(pw[:, idx4] - b, b[:, idx5])
    hidq = mxq(hid, 0, "e5m2")
    p = wbu.T @ hidq + wsu.T @ xtidx2g
    y = np.zeros((N, E))
    y[:, idx6] = p
    return y

@@ -1,0 +1,192 @@
+from contextlib import ExitStack
+
+import concourse.mybir as mybir
+
+K, T, J, R, C, N, E = 512, 2048, 256, 512, 512, 256, 1024
+FLOPS = 2 * (2 * K * R * J + R * N * J + K * N * J)
+
+P = 128
+PACK = 4
+H = J // 2
+F32 = mybir.dt.float32
+BF16 = mybir.dt.bfloat16
+I32 = mybir.dt.int32
+U32 = mybir.dt.uint32
+U16 = mybir.dt.uint16
+U8 = mybir.dt.uint8
+E2M1 = mybir.dt.float4_e2m1fn_x4
+E4M3 = mybir.dt.float8_e4m3fn_x4
+E5M2 = mybir.dt.float8_e5m2_x4
+COPY = mybir.ActivationFunctionType.Copy
+ALU = mybir.AluOpType
+
+
+def load_scale_rows(queue, plane, scales, q):
+    queue.dma_start(out=plane[32 * q : 32 * q + 4, :].bitcast(I32), in_=scales[0, 4 * q : 4 * q + 4, :].bitcast(I32))
+
+
+def load_scale_quadrant(queue, plane, scales, q):
+    rows = scales[0, 4 * q : 4 * q + 4, :].bitcast(I32)
+    queue.dma_start(
+        out=plane[32 * q : 32 * (q + 1), :].bitcast(I32), in_=rows.unsqueeze(0).broadcast_to([8, 4, rows.shape[1]])
+    )
+
+
+def tile_list_threeways_tied_skip_scattered_kernel(
+    tc, xt_words, xt_scales, w_words, w_scales, wb_words, wb_scales, ws_words, ws_scales,
+    offs, offs2, offs3, offs4, offs5, offs6, out,
+):
+    nc = tc.nc
+    with ExitStack() as ctx:
+        sb = ctx.enter_context(tc.tile_pool(name="sb", bufs=1))
+        ps = ctx.enter_context(tc.psum_pool(name="ps", bufs=1))
+
+        def tile(name, shape, dtype):
+            return sb.tile(shape, dtype, name=name, align_bytes=64)
+
+        lists = [tile("list%d" % i, [P, J // 16], U16) for i in range(6)]
+        x_words = tile("x_words", [P, T], U16)
+        x_plane = tile("x_plane", [P, T], U8)
+        w_raw = tile("w_raw", [P, R], U32)
+        w_plane_raw = tile("w_plane_raw", [P, R], U8)
+        w_codes = [tile("w_codes%d" % g, [P, 2 * P], U32) for g in range(2)]
+        w_plane = [tile("w_plane%d" % g, [P, 2 * P], U8) for g in range(2)]
+        wb_codes = tile("wb_codes", [P, N], U32)
+        wb_plane = tile("wb_plane", [P, N], U8)
+        ws_codes = tile("ws_codes", [P, N], U32)
+        ws_plane = tile("ws_plane", [P, N], U8)
+        xg_words = [tile("xg_words%d" % i, [P, J], U16) for i in range(2)]
+        xg_plane = [tile("xg_plane%d" % i, [P, J], U8) for i in range(2)]
+        a_sb = [tile("a_sb0", [P, J], F32), tile("a_sb1", [P, J], F32), tile("a_sb23", [P, 2 * J], F32)]
+        b_sb = [tile("b_sb%d" % g, [P, 2 * J], F32) for g in range(2)]
+        board = [tile("board%d" % t, [P, C], F32) for t in range(PACK)]
+        diff = tile("diff", [P, PACK, J], F32)
+        partner = [tile("partner%d" % h, [P, PACK, H], F32) for h in range(2)]
+        hid_codes = [tile("hid_codes%d" % h, [P, H], U32) for h in range(2)]
+        hid_plane = [tile("hid_plane%d" % h, [P, H], U8) for h in range(2)]
+        p_sb = [tile("p_sb%d" % h, [P, 2 * H], F32) for h in range(2)]
+        page = [tile("page%d" % u, [P, E], F32) for u in range(2)]
+
+        a_ps = [
+            ps.tile([P, J], F32, name="a_ps0"), ps.tile([P, J], F32, name="a_ps1"), ps.tile([P, 2 * J], F32, name="a_ps23")
+        ]
+        b_ps = [ps.tile([P, 2 * J], F32, name="b_ps%d" % g) for g in range(2)]
+
+        nc.vector.memset(x_plane[:].bitcast(I32), 0)
+        nc.vector.memset(ws_plane[:].bitcast(I32), 0)
+        nc.vector.memset(wb_plane[:].bitcast(I32), 0)
+        for t in range(PACK):
+            nc.vector.memset(board[t][:], 0.0)
+
+        def words_of(dram):
+            return dram[0].rearrange("p c t -> p (c t)").bitcast(I32)
+
+        nc.sync.dma_start(lists[0][:], offs)
+        nc.sync.dma_start(lists[1][:], offs2)
+        nc.sync.dma_start(out=x_words[:].bitcast(I32), in_=xt_words[0].bitcast(I32))
+        nc.sync.dma_start(out=w_raw[:].bitcast(I32), in_=words_of(w_words))
+        for q in range(4):
+            load_scale_rows(nc.sync, x_plane, xt_scales, q)
+        for q in range(4):
+            load_scale_quadrant(nc.sync if q < 2 else nc.gpsimd, w_plane_raw, w_scales, q)
+        nc.sync.dma_start(lists[2][:], offs3)
+        nc.sync.dma_start(lists[3][:], offs4)
+        nc.sync.dma_start(lists[4][:], offs5)
+        nc.sync.dma_start(out=ws_codes[:].bitcast(I32), in_=words_of(ws_words))
+        for q in range(4):
+            load_scale_rows(nc.sync, ws_plane, ws_scales, q)
+        nc.sync.dma_start(out=wb_codes[:].bitcast(I32), in_=words_of(wb_words))
+        for q in range(4):
+            load_scale_rows(nc.sync, wb_plane, wb_scales, q)
+        nc.sync.dma_start(lists[5][:], offs6)
+
+        for g in range(2):
+            nc.gpsimd.tensor_copy(
+                out=w_plane[g][:].rearrange("p (t m) -> p t m", t=2),
+                in_=w_plane_raw[:].rearrange("p (m t) -> p t m", t=PACK)[:, 2 * g : 2 * g + 2, :],
+            )
+            nc.scalar.copy(
+                out=w_codes[g][:].rearrange("p (t m) -> p m t", t=2),
+                in_=w_raw[:].rearrange("p (m t) -> p m t", t=PACK)[:, :, 2 * g : 2 * g + 2],
+            )
+        nc.gpsimd.memset(page[0][:], 0.0)
+
+        def first_stage(i, t, bank):
+            cols = slice(P * (t % 2), P * (t % 2 + 1))
+            nc.tensor.matmul_mx(
+                out=bank, lhsT=w_codes[t // 2][:, cols].bitcast(E5M2), lhsT_scale=w_plane[t // 2][:, cols],
+                rhs=xg_words[i][:].bitcast(E2M1), rhs_scale=xg_plane[i][:], start=True, stop=True,
+            )
+
+        def pair_cols(t):
+            return slice(J * (t % 2), J * (t % 2 + 1))
+
+        def half_of(i, h):
+            return lists[i][:, h * H // 16 : (h + 1) * H // 16]
+
+        for i in range(2):
+            nc.vector.tensor_copy(out=xg_plane[i][:], in_=x_plane[:].indirect(lists[i][:]))
+        for i in range(2):
+            nc.vector.tensor_copy(out=xg_words[i][:], in_=x_words[:].indirect(lists[i][:]))
+        nc.vector.memset(page[1][:], 0.0)
+        first_stage(0, 0, a_ps[0][:])
+        first_stage(0, 1, a_ps[1][:])
+        first_stage(0, 2, a_ps[2][:, :J])
+        first_stage(0, 3, a_ps[2][:, J:])
+        for t in range(PACK):
+            first_stage(1, t, b_ps[t // 2][:, pair_cols(t)])
+
+        nc.scalar.copy(out=a_sb[0][:], in_=a_ps[0][:])
+        nc.scalar.activation(out=board[0][:].indirect(lists[2][:]), in_=a_sb[0][:], func=COPY)
+        nc.vector.tensor_copy(out=a_sb[1][:], in_=a_ps[1][:])
+        nc.vector.tensor_copy(out=a_sb[2][:], in_=a_ps[2][:])
+        nc.vector.tensor_copy(out=board[1][:].indirect(lists[2][:]), in_=a_sb[1][:])
+        for t in (2, 3):
+            nc.scalar.activation(out=board[t][:].indirect(lists[2][:]), in_=a_sb[2][:, pair_cols(t)], func=COPY)
+
+        p_ps = [ps.tile([P, 2 * H], F32, name="p_ps%d" % h) for h in range(2)]
+        for h in range(2):
+            slots = slice(H * h, H * (h + 1))
+            for u in range(2):
+                cols = slice(P * u, P * (u + 1))
+                nc.tensor.matmul_mx(
+                    out=p_ps[h][:, H * u : H * (u + 1)], lhsT=ws_codes[:, cols].bitcast(E4M3), lhsT_scale=ws_plane[:, cols],
+                    rhs=xg_words[1][:, slots].bitcast(E2M1), rhs_scale=xg_plane[1][:, slots], start=(u == 0), stop=False,
+                )
+
+        for g in range(2):
+            nc.vector.tensor_copy(out=b_sb[g][:], in_=b_ps[g][:])
+        for t in range(PACK):
+            nc.vector.tensor_tensor(
+                out=diff[:, t, :], in0=board[t][:].indirect(lists[3][:]), in1=b_sb[t // 2][:, pair_cols(t)], op=ALU.subtract
+            )
+        nc.vector.tensor_copy(out=partner[1][:, 0, :], in_=b_sb[0][:, :J].indirect(half_of(4, 1)))
+        for h in range(2):
+            for t in range(h, PACK):
+                nc.scalar.activation(
+                    out=partner[h][:, t, :], in_=b_sb[t // 2][:, pair_cols(t)].indirect(half_of(4, h)), func=COPY
+                )
+
+        for h in range(2):
+            hid = sb.tile([P, H * PACK], BF16, name="hid", tag="hid", align_bytes=64)
+            nc.vector.tensor_tensor(
+                out=hid[:].rearrange("p (c i t) -> p c t i", i=4, t=PACK),
+                in0=diff[:, :, H * h : H * (h + 1)].rearrange("p t (c i) -> p c t i", i=4),
+                in1=partner[h][:].rearrange("p t (c i) -> p c t i", i=4),
+                op=ALU.max,
+            )
+            nc.vector.quantize_mx(out=hid_codes[h][:].bitcast(E5M2), scales=hid_plane[h][:], in_=hid[:])
+            for u in range(2):
+                cols = slice(P * u, P * (u + 1))
+                nc.tensor.matmul_mx(
+                    out=p_ps[h][:, H * u : H * (u + 1)], lhsT=wb_codes[:, cols].bitcast(E4M3), lhsT_scale=wb_plane[:, cols],
+                    rhs=hid_codes[h][:].bitcast(E5M2), rhs_scale=hid_plane[h][:], start=False, stop=(u == 1),
+                )
+        nc.scalar.copy(out=p_sb[0][:], in_=p_ps[0][:])
+        nc.scalar.activation(out=page[0][:].indirect(half_of(5, 0)), in_=p_sb[0][:, :H], func=COPY)
+        nc.vector.tensor_copy(out=page[1][:].indirect(half_of(5, 0)), in_=p_sb[0][:, H:])
+        nc.vector.tensor_copy(out=p_sb[1][:], in_=p_ps[1][:])
+        nc.scalar.activation(out=page[0][:].indirect(half_of(5, 1)), in_=p_sb[1][:, :H], func=COPY)
+        nc.vector.tensor_copy(out=page[1][:].indirect(half_of(5, 1)), in_=p_sb[1][:, H:])
+        for u in range(2):
+            nc.sync.dma_start(out=out[P * u : P * (u + 1), :], in_=page[u][:])

@@ -76,19 +76,21 @@ def tile_list_threeways_tied_skip_scattered_kernel(
         nc.vector.memset(ws_plane[:].bitcast(I32), 0)
         nc.vector.memset(wb_plane[:].bitcast(I32), 0)
         for t in range(PACK):
-            nc.vector.memset(board[t][:], 0.0)
+            nc.vector.memset(board[t][:].bitcast(I32), 0)
+        for u in range(2):
+            nc.gpsimd.memset(page[u][:].bitcast(I32), 0)
 
         def words_of(dram):
             return dram[0].rearrange("p c t -> p (c t)").bitcast(I32)
 
-        nc.sync.dma_start(lists[0][:], offs)
-        nc.sync.dma_start(lists[1][:], offs2)
+        for q in range(4):
+            load_scale_quadrant(nc.sync, w_plane_raw, w_scales, q)
         nc.sync.dma_start(out=x_words[:].bitcast(I32), in_=xt_words[0].bitcast(I32))
+        nc.sync.dma_start(lists[0][:], offs)
         nc.sync.dma_start(out=w_raw[:].bitcast(I32), in_=words_of(w_words))
+        nc.sync.dma_start(lists[1][:], offs2)
         for q in range(4):
             load_scale_rows(nc.sync, x_plane, xt_scales, q)
-        for q in range(4):
-            load_scale_quadrant(nc.sync if q < 2 else nc.gpsimd, w_plane_raw, w_scales, q)
         nc.sync.dma_start(lists[2][:], offs3)
         nc.sync.dma_start(lists[3][:], offs4)
         nc.sync.dma_start(lists[4][:], offs5)
@@ -101,15 +103,10 @@ def tile_list_threeways_tied_skip_scattered_kernel(
         nc.sync.dma_start(lists[5][:], offs6)
 
         for g in range(2):
-            nc.gpsimd.tensor_copy(
-                out=w_plane[g][:].rearrange("p (t m) -> p t m", t=2),
-                in_=w_plane_raw[:].rearrange("p (m t) -> p t m", t=PACK)[:, 2 * g : 2 * g + 2, :],
-            )
             nc.scalar.copy(
                 out=w_codes[g][:].rearrange("p (t m) -> p m t", t=2),
                 in_=w_raw[:].rearrange("p (m t) -> p m t", t=PACK)[:, :, 2 * g : 2 * g + 2],
             )
-        nc.gpsimd.memset(page[0][:], 0.0)
 
         def first_stage(i, t, bank):
             cols = slice(P * (t % 2), P * (t % 2 + 1))
@@ -124,11 +121,17 @@ def tile_list_threeways_tied_skip_scattered_kernel(
         def half_of(i, h):
             return lists[i][:, h * H // 16 : (h + 1) * H // 16]
 
-        for i in range(2):
-            nc.vector.tensor_copy(out=xg_plane[i][:], in_=x_plane[:].indirect(lists[i][:]))
-        for i in range(2):
+        def gather_tokens(i):
             nc.vector.tensor_copy(out=xg_words[i][:], in_=x_words[:].indirect(lists[i][:]))
-        nc.vector.memset(page[1][:], 0.0)
+            nc.vector.tensor_copy(out=xg_plane[i][:], in_=x_plane[:].indirect(lists[i][:]))
+
+        for g in range(2):
+            nc.vector.tensor_copy(
+                out=w_plane[g][:].rearrange("p (t m) -> p t m", t=2),
+                in_=w_plane_raw[:].rearrange("p (m t) -> p t m", t=PACK)[:, 2 * g : 2 * g + 2, :],
+            )
+        gather_tokens(0)
+        gather_tokens(1)
         first_stage(0, 0, a_ps[0][:])
         first_stage(0, 1, a_ps[1][:])
         first_stage(0, 2, a_ps[2][:, :J])
@@ -183,10 +186,10 @@ def tile_list_threeways_tied_skip_scattered_kernel(
                     rhs=hid_codes[h][:].bitcast(E5M2), rhs_scale=hid_plane[h][:], start=False, stop=(u == 1),
                 )
         nc.scalar.copy(out=p_sb[0][:], in_=p_ps[0][:])
-        nc.scalar.activation(out=page[0][:].indirect(half_of(5, 0)), in_=p_sb[0][:, :H], func=COPY)
-        nc.vector.tensor_copy(out=page[1][:].indirect(half_of(5, 0)), in_=p_sb[0][:, H:])
+        for u in range(2):
+            nc.scalar.activation(out=page[u][:].indirect(half_of(5, 0)), in_=p_sb[0][:, H * u : H * (u + 1)], func=COPY)
         nc.vector.tensor_copy(out=p_sb[1][:], in_=p_ps[1][:])
-        nc.scalar.activation(out=page[0][:].indirect(half_of(5, 1)), in_=p_sb[1][:, :H], func=COPY)
-        nc.vector.tensor_copy(out=page[1][:].indirect(half_of(5, 1)), in_=p_sb[1][:, H:])
+        nc.vector.tensor_copy(out=page[0][:].indirect(half_of(5, 1)), in_=p_sb[1][:, :H])
+        nc.scalar.activation(out=page[1][:].indirect(half_of(5, 1)), in_=p_sb[1][:, H:], func=COPY)
         for u in range(2):
             nc.sync.dma_start(out=out[P * u : P * (u + 1), :], in_=page[u][:])

@@ -57,28 +57,25 @@ def tile_list_threeways_tied_skip_scattered_kernel(
         ws_plane = tile("ws_plane", [P, N], U8)
         xg_words = [tile("xg_words%d" % i, [P, J], U16) for i in range(2)]
         xg_plane = [tile("xg_plane%d" % i, [P, J], U8) for i in range(2)]
-        a_sb = [tile("a_sb0", [P, J], F32), tile("a_sb1", [P, J], F32), tile("a_sb23", [P, 2 * J], F32)]
+        a_sb = [sb.tile([P, J], F32, name="a_sb%d" % t, tag="a_then_page%d" % t, align_bytes=64) for t in range(2)]
+        a_sb.extend([tile("a_sb%d" % t, [P, J], F32) for t in (2, 3)])
         b_sb = [tile("b_sb%d" % g, [P, 2 * J], F32) for g in range(2)]
         board = [tile("board%d" % t, [P, C], F32) for t in range(PACK)]
         diff = tile("diff", [P, PACK, J], F32)
         partner = [tile("partner%d" % h, [P, PACK, H], F32) for h in range(2)]
         hid_codes = [tile("hid_codes%d" % h, [P, H], U32) for h in range(2)]
         hid_plane = [tile("hid_plane%d" % h, [P, H], U8) for h in range(2)]
-        p_sb = [tile("p_sb%d" % h, [P, 2 * H], F32) for h in range(2)]
-        page = [tile("page%d" % u, [P, E], F32) for u in range(2)]
+        p_sb = [[tile("p_sb%d%d" % (u, h), [P, H], F32) for h in range(2)] for u in range(2)]
 
-        a_ps = [
-            ps.tile([P, J], F32, name="a_ps0"), ps.tile([P, J], F32, name="a_ps1"), ps.tile([P, 2 * J], F32, name="a_ps23")
-        ]
+        a_ps = [ps.tile([P, J], F32, name="a_ps%d" % t, tag="bank%d" % t) for t in range(PACK)]
         b_ps = [ps.tile([P, 2 * J], F32, name="b_ps%d" % g) for g in range(2)]
 
-        nc.vector.memset(x_plane[:].bitcast(I32), 0)
+        nc.vector.memset(x_plane[:, : T // 2].bitcast(I32), 0)
+        nc.gpsimd.memset(x_plane[:, T // 2 :].bitcast(I32), 0)
         nc.vector.memset(ws_plane[:].bitcast(I32), 0)
         nc.vector.memset(wb_plane[:].bitcast(I32), 0)
         for t in range(PACK):
-            nc.vector.memset(board[t][:].bitcast(I32), 0)
-        for u in range(2):
-            nc.gpsimd.memset(page[u][:].bitcast(I32), 0)
+            (nc.vector if t < 2 else nc.gpsimd).memset(board[t][:].bitcast(I32), 0)
 
         def words_of(dram):
             return dram[0].rearrange("p c t -> p (c t)").bitcast(I32)
@@ -87,8 +84,8 @@ def tile_list_threeways_tied_skip_scattered_kernel(
             load_scale_quadrant(nc.sync, w_plane_raw, w_scales, q)
         nc.sync.dma_start(out=x_words[:].bitcast(I32), in_=xt_words[0].bitcast(I32))
         nc.sync.dma_start(lists[0][:], offs)
-        nc.sync.dma_start(out=w_raw[:].bitcast(I32), in_=words_of(w_words))
         nc.sync.dma_start(lists[1][:], offs2)
+        nc.sync.dma_start(out=w_raw[:].bitcast(I32), in_=words_of(w_words))
         for q in range(4):
             load_scale_rows(nc.sync, x_plane, xt_scales, q)
         nc.sync.dma_start(lists[2][:], offs3)
@@ -132,10 +129,8 @@ def tile_list_threeways_tied_skip_scattered_kernel(
             )
         gather_tokens(0)
         gather_tokens(1)
-        first_stage(0, 0, a_ps[0][:])
-        first_stage(0, 1, a_ps[1][:])
-        first_stage(0, 2, a_ps[2][:, :J])
-        first_stage(0, 3, a_ps[2][:, J:])
+        for t in range(PACK):
+            first_stage(0, t, a_ps[t][:])
         for t in range(PACK):
             first_stage(1, t, b_ps[t // 2][:, pair_cols(t)])
 
@@ -144,17 +139,22 @@ def tile_list_threeways_tied_skip_scattered_kernel(
         nc.vector.tensor_copy(out=a_sb[1][:], in_=a_ps[1][:])
         nc.vector.tensor_copy(out=a_sb[2][:], in_=a_ps[2][:])
         nc.vector.tensor_copy(out=board[1][:].indirect(lists[2][:]), in_=a_sb[1][:])
+        nc.vector.tensor_copy(out=a_sb[3][:], in_=a_ps[3][:])
         for t in (2, 3):
-            nc.scalar.activation(out=board[t][:].indirect(lists[2][:]), in_=a_sb[2][:, pair_cols(t)], func=COPY)
+            nc.scalar.activation(out=board[t][:].indirect(lists[2][:]), in_=a_sb[t][:], func=COPY)
 
-        p_ps = [ps.tile([P, 2 * H], F32, name="p_ps%d" % h) for h in range(2)]
+        page = [sb.tile([P, E], F32, name="page%d" % u, tag="a_then_page%d" % u, align_bytes=64) for u in range(2)]
+        for u in range(2):
+            nc.gpsimd.memset(page[u][:].bitcast(I32), 0)
+
+        p_ps = [[ps.tile([P, H], F32, name="p_ps%d%d" % (u, h), tag="bank%d" % (u + 4 * h)) for h in range(2)] for u in range(2)]
         for h in range(2):
             slots = slice(H * h, H * (h + 1))
             for u in range(2):
                 cols = slice(P * u, P * (u + 1))
                 nc.tensor.matmul_mx(
-                    out=p_ps[h][:, H * u : H * (u + 1)], lhsT=ws_codes[:, cols].bitcast(E4M3), lhsT_scale=ws_plane[:, cols],
-                    rhs=xg_words[1][:, slots].bitcast(E2M1), rhs_scale=xg_plane[1][:, slots], start=(u == 0), stop=False,
+                    out=p_ps[u][h][:], lhsT=ws_codes[:, cols].bitcast(E4M3), lhsT_scale=ws_plane[:, cols],
+                    rhs=xg_words[1][:, slots].bitcast(E2M1), rhs_scale=xg_plane[1][:, slots], start=True, stop=False,
                 )
 
         for g in range(2):
@@ -163,9 +163,9 @@ def tile_list_threeways_tied_skip_scattered_kernel(
             nc.vector.tensor_tensor(
                 out=diff[:, t, :], in0=board[t][:].indirect(lists[3][:]), in1=b_sb[t // 2][:, pair_cols(t)], op=ALU.subtract
             )
-        nc.vector.tensor_copy(out=partner[1][:, 0, :], in_=b_sb[0][:, :J].indirect(half_of(4, 1)))
+        nc.vector.tensor_copy(out=partner[0][:, 0, :], in_=b_sb[0][:, :J].indirect(half_of(4, 0)))
         for h in range(2):
-            for t in range(h, PACK):
+            for t in range(1 - h, PACK):
                 nc.scalar.activation(
                     out=partner[h][:, t, :], in_=b_sb[t // 2][:, pair_cols(t)].indirect(half_of(4, h)), func=COPY
                 )
@@ -182,14 +182,16 @@ def tile_list_threeways_tied_skip_scattered_kernel(
             for u in range(2):
                 cols = slice(P * u, P * (u + 1))
                 nc.tensor.matmul_mx(
-                    out=p_ps[h][:, H * u : H * (u + 1)], lhsT=wb_codes[:, cols].bitcast(E4M3), lhsT_scale=wb_plane[:, cols],
-                    rhs=hid_codes[h][:].bitcast(E5M2), rhs_scale=hid_plane[h][:], start=False, stop=(u == 1),
+                    out=p_ps[u][h][:], lhsT=wb_codes[:, cols].bitcast(E4M3), lhsT_scale=wb_plane[:, cols],
+                    rhs=hid_codes[h][:].bitcast(E5M2), rhs_scale=hid_plane[h][:], start=False, stop=True,
                 )
-        nc.scalar.copy(out=p_sb[0][:], in_=p_ps[0][:])
         for u in range(2):
-            nc.scalar.activation(out=page[u][:].indirect(half_of(5, 0)), in_=p_sb[0][:, H * u : H * (u + 1)], func=COPY)
-        nc.vector.tensor_copy(out=p_sb[1][:], in_=p_ps[1][:])
-        nc.vector.tensor_copy(out=page[0][:].indirect(half_of(5, 1)), in_=p_sb[1][:, :H])
-        nc.scalar.activation(out=page[1][:].indirect(half_of(5, 1)), in_=p_sb[1][:, H:], func=COPY)
+            nc.scalar.copy(out=p_sb[u][0][:], in_=p_ps[u][0][:])
+        for u in range(2):
+            nc.scalar.activation(out=page[u][:].indirect(half_of(5, 0)), in_=p_sb[u][0][:], func=COPY)
+        for u in range(2):
+            nc.vector.tensor_copy(out=p_sb[u][1][:], in_=p_ps[u][1][:])
+        nc.vector.tensor_copy(out=page[0][:].indirect(half_of(5, 1)), in_=p_sb[0][1][:])
+        nc.scalar.activation(out=page[1][:].indirect(half_of(5, 1)), in_=p_sb[1][1][:], func=COPY)
         for u in range(2):
             nc.sync.dma_start(out=out[P * u : P * (u + 1), :], in_=page[u][:])

@@ -46,7 +46,7 @@ def tile_list_threeways_tied_skip_scattered_kernel(
 
         lists = [tile("list%d" % i, [P, J // 16], U16) for i in range(6)]
         x_words = tile("x_words", [P, T], U16)
-        x_plane = tile("x_plane", [P, T], U8)
+        x_plane = sb.tile([P, T], U8, name="x_plane", tag="plane_then_words", align_bytes=64)
         w_raw = tile("w_raw", [P, R], U32)
         w_plane_raw = tile("w_plane_raw", [P, R], U8)
         w_codes = [tile("w_codes%d" % g, [P, 2 * P], U32) for g in range(2)]
@@ -55,7 +55,7 @@ def tile_list_threeways_tied_skip_scattered_kernel(
         wb_plane = tile("wb_plane", [P, N], U8)
         ws_codes = tile("ws_codes", [P, N], U32)
         ws_plane = tile("ws_plane", [P, N], U8)
-        xg_words = [tile("xg_words%d" % i, [P, J], U16) for i in range(2)]
+        xg_words = [tile("xg_words0", [P, J], U16)]
         xg_plane = [tile("xg_plane%d" % i, [P, J], U8) for i in range(2)]
         a_sb = [sb.tile([P, J], F32, name="a_sb%d" % t, tag="a_then_page%d" % t, align_bytes=64) for t in range(2)]
         a_sb.extend([tile("a_sb%d" % t, [P, J], F32) for t in (2, 3)])
@@ -118,17 +118,16 @@ def tile_list_threeways_tied_skip_scattered_kernel(
         def half_of(i, h):
             return lists[i][:, h * H // 16 : (h + 1) * H // 16]
 
-        def gather_tokens(i):
-            nc.vector.tensor_copy(out=xg_words[i][:], in_=x_words[:].indirect(lists[i][:]))
-            nc.vector.tensor_copy(out=xg_plane[i][:], in_=x_plane[:].indirect(lists[i][:]))
-
         for g in range(2):
             nc.vector.tensor_copy(
                 out=w_plane[g][:].rearrange("p (t m) -> p t m", t=2),
                 in_=w_plane_raw[:].rearrange("p (m t) -> p t m", t=PACK)[:, 2 * g : 2 * g + 2, :],
             )
-        gather_tokens(0)
-        gather_tokens(1)
+        nc.vector.tensor_copy(out=xg_words[0][:], in_=x_words[:].indirect(lists[0][:]))
+        for i in range(2):
+            nc.vector.tensor_copy(out=xg_plane[i][:], in_=x_plane[:].indirect(lists[i][:]))
+        xg_words.append(sb.tile([P, J], U16, name="xg_words1", tag="plane_then_words", align_bytes=64))
+        nc.vector.tensor_copy(out=xg_words[1][:], in_=x_words[:].indirect(lists[1][:]))
         for t in range(PACK):
             first_stage(0, t, a_ps[t][:])
         for t in range(PACK):
@@ -163,9 +162,9 @@ def tile_list_threeways_tied_skip_scattered_kernel(
             nc.vector.tensor_tensor(
                 out=diff[:, t, :], in0=board[t][:].indirect(lists[3][:]), in1=b_sb[t // 2][:, pair_cols(t)], op=ALU.subtract
             )
-        nc.vector.tensor_copy(out=partner[0][:, 0, :], in_=b_sb[0][:, :J].indirect(half_of(4, 0)))
+        nc.vector.tensor_copy(out=partner[1][:, 0, :], in_=b_sb[0][:, :J].indirect(half_of(4, 1)))
         for h in range(2):
-            for t in range(1 - h, PACK):
+            for t in range(h, PACK):
                 nc.scalar.activation(
                     out=partner[h][:, t, :], in_=b_sb[t // 2][:, pair_cols(t)].indirect(half_of(4, h)), func=COPY
                 )

@@ -85,9 +85,9 @@ def tile_list_threeways_tied_skip_scattered_kernel(
         nc.sync.dma_start(out=x_words[:].bitcast(I32), in_=xt_words[0].bitcast(I32))
         nc.sync.dma_start(lists[0][:], offs)
         nc.sync.dma_start(lists[1][:], offs2)
-        nc.sync.dma_start(out=w_raw[:].bitcast(I32), in_=words_of(w_words))
         for q in range(4):
             load_scale_rows(nc.sync, x_plane, xt_scales, q)
+        nc.sync.dma_start(out=w_raw[:].bitcast(I32), in_=words_of(w_words))
         nc.sync.dma_start(lists[2][:], offs3)
         nc.sync.dma_start(lists[3][:], offs4)
         nc.sync.dma_start(lists[4][:], offs5)

from contextlib import ExitStack

import concourse.mybir as mybir

K, T, J, R, C, N, E = 512, 2048, 256, 512, 512, 256, 1024
FLOPS = 2 * (2 * K * R * J + R * N * J + K * N * J)

P = 128
PACK = 4
H = J // 2
F32 = mybir.dt.float32
BF16 = mybir.dt.bfloat16
I32 = mybir.dt.int32
U32 = mybir.dt.uint32
U16 = mybir.dt.uint16
U8 = mybir.dt.uint8
E2M1 = mybir.dt.float4_e2m1fn_x4
E4M3 = mybir.dt.float8_e4m3fn_x4
E5M2 = mybir.dt.float8_e5m2_x4
COPY = mybir.ActivationFunctionType.Copy
ALU = mybir.AluOpType


def load_scale_rows(queue, plane, scales, q):
    queue.dma_start(out=plane[32 * q : 32 * q + 4, :].bitcast(I32), in_=scales[0, 4 * q : 4 * q + 4, :].bitcast(I32))


def load_scale_quadrant(queue, plane, scales, q):
    rows = scales[0, 4 * q : 4 * q + 4, :].bitcast(I32)
    queue.dma_start(
        out=plane[32 * q : 32 * (q + 1), :].bitcast(I32), in_=rows.unsqueeze(0).broadcast_to([8, 4, rows.shape[1]])
    )


def tile_list_threeways_tied_skip_scattered_kernel(
    tc, xt_words, xt_scales, w_words, w_scales, wb_words, wb_scales, ws_words, ws_scales,
    offs, offs2, offs3, offs4, offs5, offs6, out,
):
    nc = tc.nc
    with ExitStack() as ctx:
        sb = ctx.enter_context(tc.tile_pool(name="sb", bufs=1))
        ps = ctx.enter_context(tc.psum_pool(name="ps", bufs=1))

        def tile(name, shape, dtype):
            return sb.tile(shape, dtype, name=name, align_bytes=64)

        lists = [tile("list%d" % i, [P, J // 16], U16) for i in range(6)]
        x_words = tile("x_words", [P, T], U16)
        x_plane = sb.tile([P, T], U8, name="x_plane", tag="plane_then_words", align_bytes=64)
        w_raw = tile("w_raw", [P, R], U32)
        w_plane_raw = tile("w_plane_raw", [P, R], U8)
        w_codes = [tile("w_codes%d" % g, [P, 2 * P], U32) for g in range(2)]
        w_plane = [tile("w_plane%d" % g, [P, 2 * P], U8) for g in range(2)]
        wb_codes = tile("wb_codes", [P, N], U32)
        wb_plane = tile("wb_plane", [P, N], U8)
        ws_codes = tile("ws_codes", [P, N], U32)
        ws_plane = tile("ws_plane", [P, N], U8)
        xg_words = [tile("xg_words0", [P, J], U16)]
        xg_plane = [tile("xg_plane%d" % i, [P, J], U8) for i in range(2)]
        a_sb = [sb.tile([P, J], F32, name="a_sb%d" % t, tag="a_then_page%d" % t, align_bytes=64) for t in range(2)]
        a_sb.extend([tile("a_sb%d" % t, [P, J], F32) for t in (2, 3)])
        b_sb = [tile("b_sb%d" % g, [P, 2 * J], F32) for g in range(2)]
        board = [tile("board%d" % t, [P, C], F32) for t in range(PACK)]
        diff = tile("diff", [P, PACK, J], F32)
        partner = [tile("partner%d" % h, [P, PACK, H], F32) for h in range(2)]
        hid_codes = [tile("hid_codes%d" % h, [P, H], U32) for h in range(2)]
        hid_plane = [tile("hid_plane%d" % h, [P, H], U8) for h in range(2)]
        p_sb = [[tile("p_sb%d%d" % (u, h), [P, H], F32) for h in range(2)] for u in range(2)]

        a_ps = [ps.tile([P, J], F32, name="a_ps%d" % t, tag="bank%d" % t) for t in range(PACK)]
        b_ps = [ps.tile([P, 2 * J], F32, name="b_ps%d" % g) for g in range(2)]

        nc.vector.memset(x_plane[:, : T // 2].bitcast(I32), 0)
        nc.gpsimd.memset(x_plane[:, T // 2 :].bitcast(I32), 0)
        nc.vector.memset(ws_plane[:].bitcast(I32), 0)
        nc.vector.memset(wb_plane[:].bitcast(I32), 0)
        for t in range(PACK):
            (nc.vector if t < 2 else nc.gpsimd).memset(board[t][:].bitcast(I32), 0)

        def words_of(dram):
            return dram[0].rearrange("p c t -> p (c t)").bitcast(I32)

        for q in range(4):
            load_scale_quadrant(nc.sync, w_plane_raw, w_scales, q)
        nc.sync.dma_start(out=x_words[:].bitcast(I32), in_=xt_words[0].bitcast(I32))
        nc.sync.dma_start(lists[0][:], offs)
        nc.sync.dma_start(lists[1][:], offs2)
        for q in range(4):
            load_scale_rows(nc.sync, x_plane, xt_scales, q)
        nc.sync.dma_start(out=w_raw[:].bitcast(I32), in_=words_of(w_words))
        nc.sync.dma_start(lists[2][:], offs3)
        nc.sync.dma_start(lists[3][:], offs4)
        nc.sync.dma_start(lists[4][:], offs5)
        nc.sync.dma_start(out=ws_codes[:].bitcast(I32), in_=words_of(ws_words))
        for q in range(4):
            load_scale_rows(nc.sync, ws_plane, ws_scales, q)
        nc.sync.dma_start(out=wb_codes[:].bitcast(I32), in_=words_of(wb_words))
        for q in range(4):
            load_scale_rows(nc.sync, wb_plane, wb_scales, q)
        nc.sync.dma_start(lists[5][:], offs6)

        for g in range(2):
            nc.scalar.copy(
                out=w_codes[g][:].rearrange("p (t m) -> p m t", t=2),
                in_=w_raw[:].rearrange("p (m t) -> p m t", t=PACK)[:, :, 2 * g : 2 * g + 2],
            )

        def first_stage(i, t, bank):
            cols = slice(P * (t % 2), P * (t % 2 + 1))
            nc.tensor.matmul_mx(
                out=bank, lhsT=w_codes[t // 2][:, cols].bitcast(E5M2), lhsT_scale=w_plane[t // 2][:, cols],
                rhs=xg_words[i][:].bitcast(E2M1), rhs_scale=xg_plane[i][:], start=True, stop=True,
            )

        def pair_cols(t):
            return slice(J * (t % 2), J * (t % 2 + 1))

        def half_of(i, h):
            return lists[i][:, h * H // 16 : (h + 1) * H // 16]

        for g in range(2):
            nc.vector.tensor_copy(
                out=w_plane[g][:].rearrange("p (t m) -> p t m", t=2),
                in_=w_plane_raw[:].rearrange("p (m t) -> p t m", t=PACK)[:, 2 * g : 2 * g + 2, :],
            )
        nc.vector.tensor_copy(out=xg_words[0][:], in_=x_words[:].indirect(lists[0][:]))
        for i in range(2):
            nc.vector.tensor_copy(out=xg_plane[i][:], in_=x_plane[:].indirect(lists[i][:]))
        xg_words.append(sb.tile([P, J], U16, name="xg_words1", tag="plane_then_words", align_bytes=64))
        nc.vector.tensor_copy(out=xg_words[1][:], in_=x_words[:].indirect(lists[1][:]))
        for t in range(PACK):
            first_stage(0, t, a_ps[t][:])
        for t in range(PACK):
            first_stage(1, t, b_ps[t // 2][:, pair_cols(t)])

        nc.scalar.copy(out=a_sb[0][:], in_=a_ps[0][:])
        nc.scalar.activation(out=board[0][:].indirect(lists[2][:]), in_=a_sb[0][:], func=COPY)
        nc.vector.tensor_copy(out=a_sb[1][:], in_=a_ps[1][:])
        nc.vector.tensor_copy(out=a_sb[2][:], in_=a_ps[2][:])
        nc.vector.tensor_copy(out=board[1][:].indirect(lists[2][:]), in_=a_sb[1][:])
        nc.vector.tensor_copy(out=a_sb[3][:], in_=a_ps[3][:])
        for t in (2, 3):
            nc.scalar.activation(out=board[t][:].indirect(lists[2][:]), in_=a_sb[t][:], func=COPY)

        page = [sb.tile([P, E], F32, name="page%d" % u, tag="a_then_page%d" % u, align_bytes=64) for u in range(2)]
        for u in range(2):
            nc.gpsimd.memset(page[u][:].bitcast(I32), 0)

        p_ps = [[ps.tile([P, H], F32, name="p_ps%d%d" % (u, h), tag="bank%d" % (u + 4 * h)) for h in range(2)] for u in range(2)]
        for h in range(2):
            slots = slice(H * h, H * (h + 1))
            for u in range(2):
                cols = slice(P * u, P * (u + 1))
                nc.tensor.matmul_mx(
                    out=p_ps[u][h][:], lhsT=ws_codes[:, cols].bitcast(E4M3), lhsT_scale=ws_plane[:, cols],
                    rhs=xg_words[1][:, slots].bitcast(E2M1), rhs_scale=xg_plane[1][:, slots], start=True, stop=False,
                )

        for g in range(2):
            nc.vector.tensor_copy(out=b_sb[g][:], in_=b_ps[g][:])
        for t in range(PACK):
            nc.vector.tensor_tensor(
                out=diff[:, t, :], in0=board[t][:].indirect(lists[3][:]), in1=b_sb[t // 2][:, pair_cols(t)], op=ALU.subtract
            )
        nc.vector.tensor_copy(out=partner[1][:, 0, :], in_=b_sb[0][:, :J].indirect(half_of(4, 1)))
        for h in range(2):
            for t in range(h, PACK):
                nc.scalar.activation(
                    out=partner[h][:, t, :], in_=b_sb[t // 2][:, pair_cols(t)].indirect(half_of(4, h)), func=COPY
                )

        for h in range(2):
            hid = sb.tile([P, H * PACK], BF16, name="hid", tag="hid", align_bytes=64)
            nc.vector.tensor_tensor(
                out=hid[:].rearrange("p (c i t) -> p c t i", i=4, t=PACK),
                in0=diff[:, :, H * h : H * (h + 1)].rearrange("p t (c i) -> p c t i", i=4),
                in1=partner[h][:].rearrange("p t (c i) -> p c t i", i=4),
                op=ALU.max,
            )
            nc.vector.quantize_mx(out=hid_codes[h][:].bitcast(E5M2), scales=hid_plane[h][:], in_=hid[:])
            for u in range(2):
                cols = slice(P * u, P * (u + 1))
                nc.tensor.matmul_mx(
                    out=p_ps[u][h][:], lhsT=wb_codes[:, cols].bitcast(E4M3), lhsT_scale=wb_plane[:, cols],
                    rhs=hid_codes[h][:].bitcast(E5M2), rhs_scale=hid_plane[h][:], start=False, stop=True,
                )
        for u in range(2):
            nc.scalar.copy(out=p_sb[u][0][:], in_=p_ps[u][0][:])
        for u in range(2):
            nc.scalar.activation(out=page[u][:].indirect(half_of(5, 0)), in_=p_sb[u][0][:], func=COPY)
        for u in range(2):
            nc.vector.tensor_copy(out=p_sb[u][1][:], in_=p_ps[u][1][:])
        nc.vector.tensor_copy(out=page[0][:].indirect(half_of(5, 1)), in_=p_sb[0][1][:])
        nc.scalar.activation(out=page[1][:].indirect(half_of(5, 1)), in_=p_sb[1][1][:], func=COPY)
        for u in range(2):
            nc.sync.dma_start(out=out[P * u : P * (u + 1), :], in_=page[u][:])
